import numpy as np
import ml_dtypes


def mxq(x, axis, fmt="e4m3"):
    dtype, down = {"e4m3": (ml_dtypes.float8_e4m3fn, 7), "e5m2": (ml_dtypes.float8_e5m2, 14)}[fmt]
    v = np.moveaxis(np.asarray(x, np.float32).astype(ml_dtypes.bfloat16).astype(np.float64), axis, -1)
    blocks = v.reshape(v.shape[:-1] + (-1, 32))
    amax = np.abs(blocks).max(-1, keepdims=True)
    byte = np.maximum(np.where(amax > 0, np.frexp(amax)[1] - 1 + 127, 0) - down, 1)
    scale = np.exp2(byte - 127.0)
    codes = (blocks / scale).astype(np.float32).astype(dtype).astype(np.float64)
    return np.moveaxis((codes * scale).reshape(v.shape), -1, axis)


WIDE = False


def mx_kscale(k):
    if not WIDE:
        return np.ones(k)
    levels = np.array([10, -10, 5, -5, 0])
    if k % 512:
        return np.exp2(np.random.permutation(np.resize(levels, k // 32))).repeat(32)
    a = np.empty((k // 512, 16))
    for p in range(k // 512):
        a[p, :8] = np.random.permutation(np.resize(levels, 8))
        for g in range(8):
            far = levels[np.abs(levels - a[p, g]) >= 10]
            a[p, g + 8] = far[np.random.randint(len(far))]
    return np.exp2(a.ravel()).repeat(32)


def f64(x):
    return np.asarray(x).astype(np.float64)


E2M1 = np.array([0.0, 0.5, 1.0, 1.5, 2.0, 3.0, 4.0, 6.0, -0.0, -0.5, -1.0, -1.5, -2.0, -3.0, -4.0, -6.0])


def pack_weight(w, fmt):
    k, n = w.shape
    w = f64(np.asarray(w, np.float32).astype(ml_dtypes.bfloat16)).reshape(k // 32, 32, n)
    amax = np.abs(w).max(1)
    if fmt == "e4m3":
        byte = np.frexp(amax)[1] - 1 + 127 - 7
    else:
        mant, ex = np.frexp(amax / 6.0)
        byte = np.where(mant > 0.5, ex, ex - 1) + 127
    byte = np.clip(np.where(amax > 0, byte, 1), 1, 254)
    scaled = (w * np.exp2(127.0 - byte)[:, None, :]).reshape(k, n).astype(np.float32)
    by_word = np.ascontiguousarray(scaled.reshape(k // 512, 128, 4, n).transpose(0, 1, 3, 2))
    if fmt == "e4m3":
        words = by_word.astype(ml_dtypes.float8_e4m3fn).view(np.uint8)
    else:
        c = by_word.astype(ml_dtypes.float4_e2m1fn).view(np.uint8) & 0xF
        words = (c[..., 0::2] | (c[..., 1::2] << 4)).reshape(k // 512, 128, 2 * n)
    return np.ascontiguousarray(words), np.ascontiguousarray(byte.astype(np.uint8).reshape(k // 512, 16, n))


def unpack_weight(words, scales, fmt):
    g, _, n = scales.shape
    words = np.ascontiguousarray(words).reshape(g, 128, n, -1)
    if fmt == "e4m3":
        vals = words.view(ml_dtypes.float8_e4m3fn).astype(np.float64)
    else:
        nib = np.empty((g, 128, n, 4), np.uint8)
        nib[..., 0::2] = words & 0xF
        nib[..., 1::2] = words >> 4
        vals = E2M1[nib]
    vals = vals * np.repeat(np.exp2(scales.astype(np.float64) - 127.0), 8, axis=1)[..., None]
    return vals.transpose(0, 1, 3, 2).reshape(g * 512, n)


K, T, R, N, B = 1024, 512, 512, 512, 128


def setup_inputs():
    n = np.random.standard_normal
    fk = mx_kscale(K)
    fr = mx_kscale(R)
    xtp = pack_weight(n((K, T)) / fk[:, None], "e4m3")
    wap = pack_weight(n((K, R)) * 1 / np.sqrt(K) * fk[:, None] * fr, "e2m1")
    wbp = pack_weight(n((R, N)) * 1 / np.sqrt(R) / fr[:, None], "e4m3")
    wyp = pack_weight(n((K, N)) * 1 / np.sqrt(K) * fk[:, None], "e2m1")
    return {
        "xt_words": xtp[0],
        "xt_scales": xtp[1],
        "wa_words": wap[0],
        "wa_scales": wap[1],
        "wb_words": wbp[0],
        "wb_scales": wbp[1],
        "wy_words": wyp[0],
        "wy_scales": wyp[1],
    }


def reference(xt_words, xt_scales, wa_words, wa_scales, wb_words, wb_scales, wy_words, wy_scales):
    xtu = unpack_weight(xt_words, xt_scales, "e4m3")
    wau = unpack_weight(wa_words, wa_scales, "e2m1")
    wbu = unpack_weight(wb_words, wb_scales, "e4m3")
    wyu = unpack_weight(wy_words, wy_scales, "e2m1")
    a = wau.T @ xtu
    m = a.reshape(R, B, T // B).mean(axis=2)
    mr = np.repeat(m, T // B, axis=1)
    hid = np.maximum(a - mr, 0.0)
    hidq = mxq(hid, 0, "e4m3")
    y = wbu.T @ hidq + wyu.T @ xtu
    return y

@@ -1,0 +1,219 @@
+from contextlib import ExitStack
+
+import concourse.mybir as mybir
+
+K, T, R, N = 1024, 512, 512, 512
+GROUP = 4
+FLOPS = 2 * K * R * T + 2 * R * N * T + 2 * K * N * T
+
+F32 = mybir.dt.float32
+BF16 = mybir.dt.bfloat16
+I32 = mybir.dt.int32
+U32 = mybir.dt.uint32
+U16 = mybir.dt.uint16
+U8 = mybir.dt.uint8
+FP8X4 = mybir.dt.float8_e4m3fn_x4
+FP4X4 = mybir.dt.float4_e2m1fn_x4
+ALU = mybir.AluOpType
+ACT = mybir.ActivationFunctionType
+
+P = 128
+PACK = 4
+PASSES = K // (P * PACK)
+TC = 128
+CHUNKS = T // TC
+N_TILES = N // P
+
+
+def load_scales(queue, plane, scales, rows):
+    by_row = scales.rearrange("z (q r) c -> r q z c", r=4)
+    for r in rows:
+        queue.dma_start(out=plane[r:P:32, :, :].bitcast(I32), in_=by_row[r].bitcast(I32))
+
+
+def tile_mix_hidden_less_group_and_skip_kernel(
+    tc, xt_words, xt_scales, wa_words, wa_scales, wb_words, wb_scales, wy_words, wy_scales, out
+):
+    nc = tc.nc
+    out_by_tile = out.rearrange("(i p) t -> p i t", p=P)
+
+    with ExitStack() as ctx:
+        keep = ctx.enter_context(tc.tile_pool(name="keep", bufs=1))
+        psum = ctx.enter_context(tc.psum_pool(name="psum", bufs=1))
+        ctx.enter_context(tc.manual_schedule())
+
+        xt = keep.tile([P, PASSES, 4 * T], U8, name="xt", align_bytes=64)
+        xt_plane = keep.tile([P, PASSES, T], U8, name="xt_plane", align_bytes=64)
+        wa_raw = keep.tile([P, PASSES, 2 * R], U8, name="wa_raw", align_bytes=64)
+        wa_plane_raw = keep.tile([P, PASSES, R], U8, name="wa_plane_raw", align_bytes=64)
+        wa_plane = keep.tile([P, PASSES, R], U8, name="wa_plane", align_bytes=64)
+        wy = keep.tile([P, PASSES, 2 * N], U8, name="wy", align_bytes=64)
+        wy_plane = keep.tile([P, PASSES, N], U8, name="wy_plane", align_bytes=64)
+        wb = keep.tile([P, 4 * N], U8, name="wb", align_bytes=64)
+        wb_plane = keep.tile([P, 1, N], U8, name="wb_plane", align_bytes=64)
+
+        nc.vector.memset(wa_plane_raw[:].bitcast(I32), 0)
+        nc.vector.memset(xt_plane[:].bitcast(I32), 0)
+        zero = keep.tile([P, 1], F32, name="zero")
+        nc.gpsimd.memset(zero[:], 0.0)
+        nc.gpsimd.memset(wy_plane[:].bitcast(I32), 0)
+        nc.gpsimd.memset(wb_plane[:].bitcast(I32), 0)
+
+        nc.sync.dma_start(out=wa_raw[:].bitcast(I32), in_=wa_words.rearrange("z p c -> p z c").bitcast(I32))
+        load_scales(nc.sync, wa_plane_raw, wa_scales, range(4))
+        nc.sync.dma_start(out=xt[:].bitcast(I32), in_=xt_words.rearrange("z p t b -> p z (t b)").bitcast(I32))
+        load_scales(nc.sync, xt_plane, xt_scales, range(4))
+        nc.sync.dma_start(out=wy[:].bitcast(I32), in_=wy_words.rearrange("z p c -> p z c").bitcast(I32))
+        load_scales(nc.sync, wy_plane, wy_scales, range(4))
+        load_scales(nc.sync, wb_plane, wb_scales, range(4))
+        nc.sync.dma_start(out=wb[:].bitcast(I32), in_=wb_words[0].rearrange("p n b -> p (n b)").bitcast(I32))
+
+        warm = keep.tile([P, 1], F32, name="warm")
+        nc.scalar.activation(out=warm[:], in_=zero[:], func=ACT.Relu)
+
+        wa = []
+        for z in range(PASSES):
+            wa_z = keep.tile([P, 2 * R], U8, name="wa_%d" % z, align_bytes=64)
+            nc.vector.tensor_copy(
+                out=wa_z[:].bitcast(U16).rearrange("p (j m) -> p j m", j=PACK),
+                in_=wa_raw[:, z, :].bitcast(U16).rearrange("p (m j) -> p j m", j=PACK),
+            )
+            wa.append(wa_z)
+            if z == 0:
+                nc.vector.tensor_copy(
+                    out=wa_plane[:].rearrange("p z (j m) -> p z j m", j=PACK),
+                    in_=wa_plane_raw[:].rearrange("p z (m j) -> p z j m", j=PACK),
+                )
+
+        def xt_pass(z, c):
+            return dict(
+                rhs=xt[:, z, 4 * TC * c : 4 * TC * (c + 1)].bitcast(FP8X4),
+                rhs_scale=xt_plane[:, z, TC * c : TC * (c + 1)],
+            )
+
+        a_bank, sums, less, hid, codes, hid_plane, y_parts = {}, {}, {}, {}, {}, {}, {}
+
+        def first_layer(c):
+            a_bank[c] = psum.tile([P, PACK, TC], F32, name="a_%d" % c, tag="a_%d" % c)
+            for z in range(PASSES):
+                for j in range(PACK):
+                    nc.tensor.matmul_mx(
+                        out=a_bank[c][:, j, :],
+                        lhsT=wa[z][:, 2 * P * j : 2 * P * (j + 1)].bitcast(FP4X4),
+                        lhsT_scale=wa_plane[:, z, P * j : P * (j + 1)],
+                        start=(z == 0 and j == 0),
+                        stop=(z == PASSES - 1 and j == PACK - 1),
+                        **xt_pass(z, c),
+                    )
+
+        def group_sums(c):
+            sums[c] = keep.tile([P, PACK * TC // GROUP], F32, name="sums_%d" % c)
+            nc.vector.tensor_reduce(
+                out=sums[c][:],
+                in_=a_bank[c][:].rearrange("p j (b i) -> p (j b) i", i=GROUP),
+                axis=mybir.AxisListType.X,
+                op=ALU.add,
+            )
+
+        def less_mean(c):
+            less[c] = keep.tile([P, PACK, TC], F32, name="less_%d" % c)
+            nc.vector.scalar_tensor_tensor(
+                out=less[c][:].rearrange("p j (b i) -> p (j b) i", i=GROUP),
+                in0=sums[c][:].unsqueeze(2).to_broadcast([P, PACK * TC // GROUP, GROUP]),
+                scalar=-1.0 / GROUP,
+                in1=a_bank[c][:].rearrange("p j (b i) -> p (j b) i", i=GROUP),
+                op0=ALU.mult,
+                op1=ALU.add,
+            )
+
+        def relu(c, on_vector):
+            hid[c] = keep.tile([P, TC, PACK], BF16, name="hid_%d" % c, align_bytes=64)
+            src = less[c][:].rearrange("p j t -> p t j")
+            if on_vector:
+                nc.vector.tensor_scalar_max(out=hid[c][:], in0=src, scalar1=0.0)
+            else:
+                nc.scalar.activation(out=hid[c][:], in_=src, func=ACT.Relu)
+
+        def quantize(c):
+            codes[c] = keep.tile([P, TC], U32, name="codes_%d" % c, align_bytes=64)
+            hid_plane[c] = keep.tile([P, TC], U8, name="hid_plane_%d" % c, align_bytes=64)
+            nc.vector.quantize_mx(
+                out=codes[c][:].bitcast(FP8X4),
+                scales=hid_plane[c][:],
+                in_=hid[c][:].rearrange("p t j -> p (t j)"),
+            )
+
+        def skip(c, tags):
+            per_bank = N_TILES // len(tags)
+            y_parts[c] = []
+            for h, tag in enumerate(tags):
+                bank = psum.tile([P, PACK, TC], F32, name="y_%d_%d" % (c, h), tag=tag)
+                tiles = range(per_bank * h, per_bank * (h + 1))
+                y_parts[c].append((bank, tiles))
+                for z in range(PASSES):
+                    for i in tiles:
+                        nc.tensor.matmul_mx(
+                            out=bank[:, i - tiles[0], :],
+                            lhsT=wy[:, z, 2 * P * i : 2 * P * (i + 1)].bitcast(FP4X4),
+                            lhsT_scale=wy_plane[:, z, P * i : P * (i + 1)],
+                            start=(z == 0 and i == tiles[0]),
+                            stop=False,
+                            **xt_pass(z, c),
+                        )
+
+        def second_layer(c):
+            for bank, tiles in y_parts[c]:
+                for i in tiles:
+                    nc.tensor.matmul_mx(
+                        out=bank[:, i - tiles[0], :],
+                        lhsT=wb[:, 4 * P * i : 4 * P * (i + 1)].bitcast(FP8X4),
+                        lhsT_scale=wb_plane[:, 0, P * i : P * (i + 1)],
+                        rhs=codes[c][:].bitcast(FP8X4),
+                        rhs_scale=hid_plane[c][:],
+                        start=False,
+                        stop=(i == tiles[-1]),
+                    )
+
+        def store(c):
+            for h, (bank, tiles) in enumerate(y_parts[c]):
+                res = keep.tile([P, len(tiles), TC], F32, name="res_%d_%d" % (c, h))
+                if h == 0:
+                    nc.scalar.copy(out=res[:], in_=bank[:, 0 : len(tiles), :])
+                    queue = nc.sync
+                else:
+                    nc.vector.tensor_copy(out=res[:], in_=bank[:, 0 : len(tiles), :])
+                    queue = nc.sync
+                queue.dma_start(
+                    out=out_by_tile[:, tiles[0] : tiles[-1] + 1, TC * c : TC * (c + 1)], in_=res[:]
+                )
+
+        for c in range(CHUNKS):
+            first_layer(c)
+        group_sums(0)
+        less_mean(0)
+        relu(0, False)
+        skip(0, ["y_0"])
+        skip(1, ["y_1"])
+        group_sums(1)
+        group_sums(2)
+        less_mean(1)
+        relu(1, False)
+        quantize(0)
+        second_layer(0)
+        store(0)
+        skip(2, ["y_2"])
+        group_sums(3)
+        less_mean(2)
+        relu(2, False)
+        quantize(1)
+        second_layer(1)
+        store(1)
+        skip(3, ["y_3", "a_0"])
+        less_mean(3)
+        quantize(2)
+        second_layer(2)
+        store(2)
+        relu(3, True)
+        quantize(3)
+        second_layer(3)
+        store(3)

@@ -55,9 +55,9 @@ def tile_mix_hidden_less_group_and_skip_kernel(
         nc.vector.memset(wa_plane_raw[:].bitcast(I32), 0)
         nc.vector.memset(xt_plane[:].bitcast(I32), 0)
         zero = keep.tile([P, 1], F32, name="zero")
-        nc.gpsimd.memset(zero[:], 0.0)
-        nc.gpsimd.memset(wy_plane[:].bitcast(I32), 0)
-        nc.gpsimd.memset(wb_plane[:].bitcast(I32), 0)
+        nc.vector.memset(zero[:], 0.0)
+        nc.vector.memset(wy_plane[:].bitcast(I32), 0)
+        nc.vector.memset(wb_plane[:].bitcast(I32), 0)
 
         nc.sync.dma_start(out=wa_raw[:].bitcast(I32), in_=wa_words.rearrange("z p c -> p z c").bitcast(I32))
         load_scales(nc.sync, wa_plane_raw, wa_scales, range(4))
@@ -93,73 +93,77 @@ def tile_mix_hidden_less_group_and_skip_kernel(
 
         a_bank, sums, less, hid, codes, hid_plane, y_parts = {}, {}, {}, {}, {}, {}, {}
 
-        def first_layer(c):
-            a_bank[c] = psum.tile([P, PACK, TC], F32, name="a_%d" % c, tag="a_%d" % c)
+        def first_layer(c, slots):
+            bank = psum.tile([P, PACK, TC], F32, name="a_%d_%d" % (c, slots[0]), tag="a_%d_%d" % (c, slots[0]))
+            a_bank[c, slots[0]] = bank[:, 0 : len(slots), :].rearrange("p j (b i) -> p (j b) i", i=GROUP)
             for z in range(PASSES):
-                for j in range(PACK):
+                for j in slots:
                     nc.tensor.matmul_mx(
-                        out=a_bank[c][:, j, :],
+                        out=bank[:, j - slots[0], :],
                         lhsT=wa[z][:, 2 * P * j : 2 * P * (j + 1)].bitcast(FP4X4),
                         lhsT_scale=wa_plane[:, z, P * j : P * (j + 1)],
-                        start=(z == 0 and j == 0),
-                        stop=(z == PASSES - 1 and j == PACK - 1),
+                        start=(z == 0 and j == slots[0]),
+                        stop=(z == PASSES - 1 and j == slots[-1]),
                         **xt_pass(z, c),
                     )
 
-        def group_sums(c):
-            sums[c] = keep.tile([P, PACK * TC // GROUP], F32, name="sums_%d" % c)
-            nc.vector.tensor_reduce(
-                out=sums[c][:],
-                in_=a_bank[c][:].rearrange("p j (b i) -> p (j b) i", i=GROUP),
-                axis=mybir.AxisListType.X,
-                op=ALU.add,
-            )
+        def group_sums(c, slots):
+            key = (c, slots[0])
+            sums[key] = keep.tile([P, len(slots) * TC // GROUP], F32, name="sums_%d_%d" % key)
+            nc.vector.tensor_reduce(out=sums[key][:], in_=a_bank[key], axis=mybir.AxisListType.X, op=ALU.add)
 
-        def less_mean(c):
-            less[c] = keep.tile([P, PACK, TC], F32, name="less_%d" % c)
+        def less_mean(c, slots):
+            key = (c, slots[0])
+            if slots[0] == 0:
+                less[c] = keep.tile([P, PACK, TC], F32, name="less_%d" % c)
             nc.vector.scalar_tensor_tensor(
-                out=less[c][:].rearrange("p j (b i) -> p (j b) i", i=GROUP),
-                in0=sums[c][:].unsqueeze(2).to_broadcast([P, PACK * TC // GROUP, GROUP]),
+                out=less[c][:, slots[0] : slots[-1] + 1, :].rearrange("p j (b i) -> p (j b) i", i=GROUP),
+                in0=sums[key][:].unsqueeze(2).to_broadcast([P, len(slots) * TC // GROUP, GROUP]),
                 scalar=-1.0 / GROUP,
-                in1=a_bank[c][:].rearrange("p j (b i) -> p (j b) i", i=GROUP),
+                in1=a_bank[key],
                 op0=ALU.mult,
                 op1=ALU.add,
             )
 
-        def relu(c, on_vector):
+        def relu(c):
             hid[c] = keep.tile([P, TC, PACK], BF16, name="hid_%d" % c, align_bytes=64)
-            src = less[c][:].rearrange("p j t -> p t j")
-            if on_vector:
-                nc.vector.tensor_scalar_max(out=hid[c][:], in0=src, scalar1=0.0)
-            else:
-                nc.scalar.activation(out=hid[c][:], in_=src, func=ACT.Relu)
+            nc.scalar.activation(out=hid[c][:], in_=less[c][:].rearrange("p j t -> p t j"), func=ACT.Relu)
 
-        def quantize(c):
+        def relu_on_vector(c, halves):
+            hid[c] = keep.tile([P, TC, PACK], BF16, name="hid_%d" % c, align_bytes=64)
+            for cols in halves:
+                nc.vector.tensor_scalar_max(
+                    out=hid[c][:, cols, :], in0=less[c][:, :, cols].rearrange("p j t -> p t j"), scalar1=0.0
+                )
+
+        def quantize(c, parts):
             codes[c] = keep.tile([P, TC], U32, name="codes_%d" % c, align_bytes=64)
             hid_plane[c] = keep.tile([P, TC], U8, name="hid_plane_%d" % c, align_bytes=64)
-            nc.vector.quantize_mx(
-                out=codes[c][:].bitcast(FP8X4),
-                scales=hid_plane[c][:],
-                in_=hid[c][:].rearrange("p t j -> p (t j)"),
-            )
+            for cols in parts:
+                nc.vector.quantize_mx(
+                    out=codes[c][:, cols].bitcast(FP8X4),
+                    scales=hid_plane[c][:, cols],
+                    in_=hid[c][:, cols, :].rearrange("p t j -> p (t j)"),
+                )
 
-        def skip(c, tags):
+        def open_result(c, tags):
             per_bank = N_TILES // len(tags)
             y_parts[c] = []
             for h, tag in enumerate(tags):
                 bank = psum.tile([P, PACK, TC], F32, name="y_%d_%d" % (c, h), tag=tag)
-                tiles = range(per_bank * h, per_bank * (h + 1))
-                y_parts[c].append((bank, tiles))
-                for z in range(PASSES):
-                    for i in tiles:
-                        nc.tensor.matmul_mx(
-                            out=bank[:, i - tiles[0], :],
-                            lhsT=wy[:, z, 2 * P * i : 2 * P * (i + 1)].bitcast(FP4X4),
-                            lhsT_scale=wy_plane[:, z, P * i : P * (i + 1)],
-                            start=(z == 0 and i == tiles[0]),
-                            stop=False,
-                            **xt_pass(z, c),
-                        )
+                y_parts[c].append((bank, range(per_bank * h, per_bank * (h + 1))))
+
+        def skip(c, z):
+            for bank, tiles in y_parts[c]:
+                for i in tiles:
+                    nc.tensor.matmul_mx(
+                        out=bank[:, i - tiles[0], :],
+                        lhsT=wy[:, z, 2 * P * i : 2 * P * (i + 1)].bitcast(FP4X4),
+                        lhsT_scale=wy_plane[:, z, P * i : P * (i + 1)],
+                        start=(z == 0 and i == tiles[0]),
+                        stop=False,
+                        **xt_pass(z, c),
+                    )
 
         def second_layer(c):
             for bank, tiles in y_parts[c]:
@@ -175,45 +179,66 @@ def tile_mix_hidden_less_group_and_skip_kernel(
                     )
 
         def store(c):
-            for h, (bank, tiles) in enumerate(y_parts[c]):
-                res = keep.tile([P, len(tiles), TC], F32, name="res_%d_%d" % (c, h))
-                if h == 0:
-                    nc.scalar.copy(out=res[:], in_=bank[:, 0 : len(tiles), :])
-                    queue = nc.sync
-                else:
-                    nc.vector.tensor_copy(out=res[:], in_=bank[:, 0 : len(tiles), :])
-                    queue = nc.sync
-                queue.dma_start(
-                    out=out_by_tile[:, tiles[0] : tiles[-1] + 1, TC * c : TC * (c + 1)], in_=res[:]
-                )
+            bank, tiles = y_parts[c][0]
+            res = keep.tile([P, N_TILES, TC], F32, name="res_%d" % c)
+            nc.scalar.copy(out=res[:], in_=bank[:])
+            nc.sync.dma_start(out=out_by_tile[:, :, TC * c : TC * (c + 1)], in_=res[:])
 
-        for c in range(CHUNKS):
-            first_layer(c)
-        group_sums(0)
-        less_mean(0)
-        relu(0, False)
-        skip(0, ["y_0"])
-        skip(1, ["y_1"])
-        group_sums(1)
-        group_sums(2)
-        less_mean(1)
-        relu(1, False)
-        quantize(0)
+        def store_last(c):
+            for h in range(2):
+                res = keep.tile([P, 2, TC], F32, name="res_%d_%d" % (c, h))
+                for u in range(2):
+                    bank, tiles = y_parts[c][2 * u + h]
+                    if h == 0:
+                        nc.scalar.copy(out=res[:, u, :], in_=bank[:, 0, :])
+                    else:
+                        nc.vector.tensor_copy(out=res[:, u, :], in_=bank[:, 0, :])
+                queue = nc.scalar if h == 0 else nc.sync
+                queue.dma_start(out=out_by_tile[:, h:N_TILES:2, TC * c : TC * (c + 1)], in_=res[:])
+
+        all_cols = [slice(0, TC)]
+        halves = [slice(0, TC // 2), slice(TC // 2, TC)]
+        low, high, whole = range(0, 2), range(2, 4), range(4)
+        first_layer(0, low)
+        first_layer(0, high)
+        first_layer(1, whole)
+        first_layer(2, whole)
+        open_result(0, ["y_0"])
+        skip(0, 0)
+        skip(0, 1)
+        first_layer(3, whole)
+        group_sums(0, low)
+        less_mean(0, low)
+        group_sums(0, high)
+        less_mean(0, high)
+        relu(0)
+        group_sums(1, whole)
+        less_mean(1, whole)
+        relu(1)
+        group_sums(2, whole)
+        quantize(0, all_cols)
         second_layer(0)
         store(0)
-        skip(2, ["y_2"])
-        group_sums(3)
-        less_mean(2)
-        relu(2, False)
-        quantize(1)
+        less_mean(2, whole)
+        relu(2)
+        open_result(1, ["y_1"])
+        skip(1, 0)
+        skip(1, 1)
+        open_result(2, ["y_2"])
+        skip(2, 0)
+        group_sums(3, whole)
+        quantize(1, all_cols)
         second_layer(1)
         store(1)
-        skip(3, ["y_3", "a_0"])
-        less_mean(3)
-        quantize(2)
+        skip(2, 1)
+        less_mean(3, whole)
+        quantize(2, all_cols)
         second_layer(2)
         store(2)
-        relu(3, True)
-        quantize(3)
+        open_result(3, ["a_0_0", "a_0_2", "a_1_0", "a_2_0"])
+        skip(3, 0)
+        skip(3, 1)
+        relu_on_vector(3, halves)
+        quantize(3, halves)
         second_layer(3)
-        store(3)
+        store_last(3)

@@ -179,22 +179,14 @@ def tile_mix_hidden_less_group_and_skip_kernel(
                     )
 
         def store(c):
-            bank, tiles = y_parts[c][0]
-            res = keep.tile([P, N_TILES, TC], F32, name="res_%d" % c)
-            nc.scalar.copy(out=res[:], in_=bank[:])
-            nc.sync.dma_start(out=out_by_tile[:, :, TC * c : TC * (c + 1)], in_=res[:])
-
-        def store_last(c):
-            for h in range(2):
-                res = keep.tile([P, 2, TC], F32, name="res_%d_%d" % (c, h))
-                for u in range(2):
-                    bank, tiles = y_parts[c][2 * u + h]
-                    if h == 0:
-                        nc.scalar.copy(out=res[:, u, :], in_=bank[:, 0, :])
-                    else:
-                        nc.vector.tensor_copy(out=res[:, u, :], in_=bank[:, 0, :])
-                queue = nc.scalar if h == 0 else nc.sync
-                queue.dma_start(out=out_by_tile[:, h:N_TILES:2, TC * c : TC * (c + 1)], in_=res[:])
+            for h, (bank, tiles) in enumerate(y_parts[c]):
+                res = keep.tile([P, len(tiles), TC], F32, name="res_%d_%d" % (c, h))
+                if h % 2 == 0:
+                    nc.scalar.copy(out=res[:], in_=bank[:, 0 : len(tiles), :])
+                else:
+                    nc.vector.tensor_copy(out=res[:], in_=bank[:, 0 : len(tiles), :])
+                queue = nc.scalar if h == 2 else nc.sync
+                queue.dma_start(out=out_by_tile[:, tiles[0] : tiles[-1] + 1, TC * c : TC * (c + 1)], in_=res[:])
 
         all_cols = [slice(0, TC)]
         halves = [slice(0, TC // 2), slice(TC // 2, TC)]
@@ -203,42 +195,42 @@ def tile_mix_hidden_less_group_and_skip_kernel(
         first_layer(0, high)
         first_layer(1, whole)
         first_layer(2, whole)
+        first_layer(3, whole)
         open_result(0, ["y_0"])
         skip(0, 0)
         skip(0, 1)
-        first_layer(3, whole)
         group_sums(0, low)
-        less_mean(0, low)
         group_sums(0, high)
+        less_mean(0, low)
         less_mean(0, high)
         relu(0)
         group_sums(1, whole)
-        less_mean(1, whole)
-        relu(1)
-        group_sums(2, whole)
         quantize(0, all_cols)
         second_layer(0)
+        less_mean(1, whole)
+        relu(1)
         store(0)
-        less_mean(2, whole)
-        relu(2)
         open_result(1, ["y_1"])
         skip(1, 0)
         skip(1, 1)
-        open_result(2, ["y_2"])
+        open_result(2, ["y_2", "a_0_0"])
         skip(2, 0)
+        skip(2, 1)
+        group_sums(2, whole)
         group_sums(3, whole)
+        less_mean(2, whole)
+        relu(2)
         quantize(1, all_cols)
         second_layer(1)
         store(1)
-        skip(2, 1)
+        open_result(3, ["a_0_2", "a_1_0", "a_2_0", "y_0"])
+        skip(3, 0)
+        skip(3, 1)
         less_mean(3, whole)
         quantize(2, all_cols)
         second_layer(2)
-        store(2)
-        open_result(3, ["a_0_0", "a_0_2", "a_1_0", "a_2_0"])
-        skip(3, 0)
-        skip(3, 1)
         relu_on_vector(3, halves)
         quantize(3, halves)
         second_layer(3)
-        store_last(3)
+        store(2)
+        store(3)

@@ -54,8 +54,6 @@ def tile_mix_hidden_less_group_and_skip_kernel(
 
         nc.vector.memset(wa_plane_raw[:].bitcast(I32), 0)
         nc.vector.memset(xt_plane[:].bitcast(I32), 0)
-        zero = keep.tile([P, 1], F32, name="zero")
-        nc.vector.memset(zero[:], 0.0)
         nc.vector.memset(wy_plane[:].bitcast(I32), 0)
         nc.vector.memset(wb_plane[:].bitcast(I32), 0)
 
@@ -68,8 +66,6 @@ def tile_mix_hidden_less_group_and_skip_kernel(
         load_scales(nc.sync, wb_plane, wb_scales, range(4))
         nc.sync.dma_start(out=wb[:].bitcast(I32), in_=wb_words[0].rearrange("p n b -> p (n b)").bitcast(I32))
 
-        warm = keep.tile([P, 1], F32, name="warm")
-        nc.scalar.activation(out=warm[:], in_=zero[:], func=ACT.Relu)
 
         wa = []
         for z in range(PASSES):
@@ -111,6 +107,15 @@ def tile_mix_hidden_less_group_and_skip_kernel(
             key = (c, slots[0])
             sums[key] = keep.tile([P, len(slots) * TC // GROUP], F32, name="sums_%d_%d" % key)
             nc.vector.tensor_reduce(out=sums[key][:], in_=a_bank[key], axis=mybir.AxisListType.X, op=ALU.add)
+
+        def group_sums_by_halves(c):
+            groups = PACK * TC // GROUP
+            by_member = keep.tile([P, GROUP, groups], F32, name="by_member_%d" % c)
+            nc.scalar.copy(out=by_member[:], in_=a_bank[c, 0].rearrange("p g i -> p i g"))
+            pairs = keep.tile([P, 2, groups], F32, name="pairs_%d" % c)
+            nc.gpsimd.tensor_add(out=pairs[:], in0=by_member[:, 0:2, :], in1=by_member[:, 2:4, :])
+            sums[c, 0] = keep.tile([P, groups], F32, name="sums_%d_0" % c)
+            nc.gpsimd.tensor_add(out=sums[c, 0][:], in0=pairs[:, 0, :], in1=pairs[:, 1, :])
 
         def less_mean(c, slots):
             key = (c, slots[0])
@@ -194,8 +199,8 @@ def tile_mix_hidden_less_group_and_skip_kernel(
         first_layer(0, low)
         first_layer(0, high)
         first_layer(1, whole)
-        first_layer(2, whole)
         first_layer(3, whole)
+        first_layer(2, whole)
         open_result(0, ["y_0"])
         skip(0, 0)
         skip(0, 1)
@@ -204,6 +209,7 @@ def tile_mix_hidden_less_group_and_skip_kernel(
         less_mean(0, low)
         less_mean(0, high)
         relu(0)
+        group_sums_by_halves(3)
         group_sums(1, whole)
         quantize(0, all_cols)
         second_layer(0)
@@ -217,7 +223,6 @@ def tile_mix_hidden_less_group_and_skip_kernel(
         skip(2, 0)
         skip(2, 1)
         group_sums(2, whole)
-        group_sums(3, whole)
         less_mean(2, whole)
         relu(2)
         quantize(1, all_cols)

@@ -111,7 +111,12 @@ def tile_mix_hidden_less_group_and_skip_kernel(
         def group_sums_by_halves(c):
             groups = PACK * TC // GROUP
             by_member = keep.tile([P, GROUP, groups], F32, name="by_member_%d" % c)
-            nc.scalar.copy(out=by_member[:], in_=a_bank[c, 0].rearrange("p g i -> p i g"))
+            nc.scalar.activation(
+                out=by_member[:].rearrange("p i (b j) -> p i b j", j=PACK),
+                in_=a_bank[c, 0].rearrange("p (j b) i -> p i b j", j=PACK),
+                func=ACT.Copy,
+                scale=-1.0 / GROUP,
+            )
             pairs = keep.tile([P, 2, groups], F32, name="pairs_%d" % c)
             nc.gpsimd.tensor_add(out=pairs[:], in0=by_member[:, 0:2, :], in1=by_member[:, 2:4, :])
             sums[c, 0] = keep.tile([P, groups], F32, name="sums_%d_0" % c)
@@ -134,12 +139,20 @@ def tile_mix_hidden_less_group_and_skip_kernel(
             hid[c] = keep.tile([P, TC, PACK], BF16, name="hid_%d" % c, align_bytes=64)
             nc.scalar.activation(out=hid[c][:], in_=less[c][:].rearrange("p j t -> p t j"), func=ACT.Relu)
 
-        def relu_on_vector(c, halves):
-            hid[c] = keep.tile([P, TC, PACK], BF16, name="hid_%d" % c, align_bytes=64)
-            for cols in halves:
-                nc.vector.tensor_scalar_max(
-                    out=hid[c][:, cols, :], in0=less[c][:, :, cols].rearrange("p j t -> p t j"), scalar1=0.0
-                )
+        def less_mean_packed(c, cols):
+            groups = slice(cols.start // GROUP, cols.stop // GROUP)
+            count = groups.stop - groups.start
+            nc.vector.tensor_tensor(
+                out=less[c][:, cols, :].rearrange("p (b i) j -> p b i j", i=GROUP),
+                in0=a_bank[c, 0].rearrange("p (j b) i -> p b i j", j=PACK)[:, groups, :, :],
+                in1=sums[c, 0][:].rearrange("p (b j) -> p b j", j=PACK)[:, groups, :]
+                .unsqueeze(2)
+                .to_broadcast([P, count, GROUP, PACK]),
+                op=ALU.add,
+            )
+
+        def relu_packed(c, cols):
+            nc.vector.tensor_scalar_max(out=hid[c][:, cols, :], in0=less[c][:, cols, :], scalar1=0.0)
 
         def quantize(c, parts):
             codes[c] = keep.tile([P, TC], U32, name="codes_%d" % c, align_bytes=64)
@@ -231,10 +244,14 @@ def tile_mix_hidden_less_group_and_skip_kernel(
         open_result(3, ["a_0_2", "a_1_0", "a_2_0", "y_0"])
         skip(3, 0)
         skip(3, 1)
-        less_mean(3, whole)
+        less[3] = keep.tile([P, TC, PACK], BF16, name="less_3", align_bytes=64)
+        hid[3] = keep.tile([P, TC, PACK], BF16, name="hid_3", align_bytes=64)
+        less_mean_packed(3, halves[0])
+        less_mean_packed(3, halves[1])
+        relu_packed(3, halves[0])
         quantize(2, all_cols)
         second_layer(2)
-        relu_on_vector(3, halves)
+        relu_packed(3, halves[1])
         quantize(3, halves)
         second_layer(3)
         store(2)

from contextlib import ExitStack

import concourse.mybir as mybir

K, T, R, N = 1024, 512, 512, 512
GROUP = 4
FLOPS = 2 * K * R * T + 2 * R * N * T + 2 * K * N * T

F32 = mybir.dt.float32
BF16 = mybir.dt.bfloat16
I32 = mybir.dt.int32
U32 = mybir.dt.uint32
U16 = mybir.dt.uint16
U8 = mybir.dt.uint8
FP8X4 = mybir.dt.float8_e4m3fn_x4
FP4X4 = mybir.dt.float4_e2m1fn_x4
ALU = mybir.AluOpType
ACT = mybir.ActivationFunctionType

P = 128
PACK = 4
PASSES = K // (P * PACK)
TC = 128
CHUNKS = T // TC
N_TILES = N // P


def load_scales(queue, plane, scales, rows):
    by_row = scales.rearrange("z (q r) c -> r q z c", r=4)
    for r in rows:
        queue.dma_start(out=plane[r:P:32, :, :].bitcast(I32), in_=by_row[r].bitcast(I32))


def tile_mix_hidden_less_group_and_skip_kernel(
    tc, xt_words, xt_scales, wa_words, wa_scales, wb_words, wb_scales, wy_words, wy_scales, out
):
    nc = tc.nc
    out_by_tile = out.rearrange("(i p) t -> p i t", p=P)

    with ExitStack() as ctx:
        keep = ctx.enter_context(tc.tile_pool(name="keep", bufs=1))
        psum = ctx.enter_context(tc.psum_pool(name="psum", bufs=1))
        ctx.enter_context(tc.manual_schedule())

        xt = keep.tile([P, PASSES, 4 * T], U8, name="xt", align_bytes=64)
        xt_plane = keep.tile([P, PASSES, T], U8, name="xt_plane", align_bytes=64)
        wa_raw = keep.tile([P, PASSES, 2 * R], U8, name="wa_raw", align_bytes=64)
        wa_plane_raw = keep.tile([P, PASSES, R], U8, name="wa_plane_raw", align_bytes=64)
        wa_plane = keep.tile([P, PASSES, R], U8, name="wa_plane", align_bytes=64)
        wy = keep.tile([P, PASSES, 2 * N], U8, name="wy", align_bytes=64)
        wy_plane = keep.tile([P, PASSES, N], U8, name="wy_plane", align_bytes=64)
        wb = keep.tile([P, 4 * N], U8, name="wb", align_bytes=64)
        wb_plane = keep.tile([P, 1, N], U8, name="wb_plane", align_bytes=64)

        nc.vector.memset(wa_plane_raw[:].bitcast(I32), 0)
        nc.vector.memset(xt_plane[:].bitcast(I32), 0)
        nc.vector.memset(wy_plane[:].bitcast(I32), 0)
        nc.vector.memset(wb_plane[:].bitcast(I32), 0)

        nc.sync.dma_start(out=wa_raw[:].bitcast(I32), in_=wa_words.rearrange("z p c -> p z c").bitcast(I32))
        load_scales(nc.sync, wa_plane_raw, wa_scales, range(4))
        nc.sync.dma_start(out=xt[:].bitcast(I32), in_=xt_words.rearrange("z p t b -> p z (t b)").bitcast(I32))
        load_scales(nc.sync, xt_plane, xt_scales, range(4))
        nc.sync.dma_start(out=wy[:].bitcast(I32), in_=wy_words.rearrange("z p c -> p z c").bitcast(I32))
        load_scales(nc.sync, wy_plane, wy_scales, range(4))
        load_scales(nc.sync, wb_plane, wb_scales, range(4))
        nc.sync.dma_start(out=wb[:].bitcast(I32), in_=wb_words[0].rearrange("p n b -> p (n b)").bitcast(I32))


        wa = []
        for z in range(PASSES):
            wa_z = keep.tile([P, 2 * R], U8, name="wa_%d" % z, align_bytes=64)
            nc.vector.tensor_copy(
                out=wa_z[:].bitcast(U16).rearrange("p (j m) -> p j m", j=PACK),
                in_=wa_raw[:, z, :].bitcast(U16).rearrange("p (m j) -> p j m", j=PACK),
            )
            wa.append(wa_z)
            if z == 0:
                nc.vector.tensor_copy(
                    out=wa_plane[:].rearrange("p z (j m) -> p z j m", j=PACK),
                    in_=wa_plane_raw[:].rearrange("p z (m j) -> p z j m", j=PACK),
                )

        def xt_pass(z, c):
            return dict(
                rhs=xt[:, z, 4 * TC * c : 4 * TC * (c + 1)].bitcast(FP8X4),
                rhs_scale=xt_plane[:, z, TC * c : TC * (c + 1)],
            )

        a_bank, sums, less, hid, codes, hid_plane, y_parts = {}, {}, {}, {}, {}, {}, {}

        def first_layer(c, slots):
            bank = psum.tile([P, PACK, TC], F32, name="a_%d_%d" % (c, slots[0]), tag="a_%d_%d" % (c, slots[0]))
            a_bank[c, slots[0]] = bank[:, 0 : len(slots), :].rearrange("p j (b i) -> p (j b) i", i=GROUP)
            for z in range(PASSES):
                for j in slots:
                    nc.tensor.matmul_mx(
                        out=bank[:, j - slots[0], :],
                        lhsT=wa[z][:, 2 * P * j : 2 * P * (j + 1)].bitcast(FP4X4),
                        lhsT_scale=wa_plane[:, z, P * j : P * (j + 1)],
                        start=(z == 0 and j == slots[0]),
                        stop=(z == PASSES - 1 and j == slots[-1]),
                        **xt_pass(z, c),
                    )

        def group_sums(c, slots):
            key = (c, slots[0])
            sums[key] = keep.tile([P, len(slots) * TC // GROUP], F32, name="sums_%d_%d" % key)
            nc.vector.tensor_reduce(out=sums[key][:], in_=a_bank[key], axis=mybir.AxisListType.X, op=ALU.add)

        def group_sums_by_halves(c):
            groups = PACK * TC // GROUP
            by_member = keep.tile([P, GROUP, groups], F32, name="by_member_%d" % c)
            nc.scalar.activation(
                out=by_member[:].rearrange("p i (b j) -> p i b j", j=PACK),
                in_=a_bank[c, 0].rearrange("p (j b) i -> p i b j", j=PACK),
                func=ACT.Copy,
                scale=-1.0 / GROUP,
            )
            pairs = keep.tile([P, 2, groups], F32, name="pairs_%d" % c)
            nc.gpsimd.tensor_add(out=pairs[:], in0=by_member[:, 0:2, :], in1=by_member[:, 2:4, :])
            sums[c, 0] = keep.tile([P, groups], F32, name="sums_%d_0" % c)
            nc.gpsimd.tensor_add(out=sums[c, 0][:], in0=pairs[:, 0, :], in1=pairs[:, 1, :])

        def less_mean(c, slots):
            key = (c, slots[0])
            if slots[0] == 0:
                less[c] = keep.tile([P, PACK, TC], F32, name="less_%d" % c)
            nc.vector.scalar_tensor_tensor(
                out=less[c][:, slots[0] : slots[-1] + 1, :].rearrange("p j (b i) -> p (j b) i", i=GROUP),
                in0=sums[key][:].unsqueeze(2).to_broadcast([P, len(slots) * TC // GROUP, GROUP]),
                scalar=-1.0 / GROUP,
                in1=a_bank[key],
                op0=ALU.mult,
                op1=ALU.add,
            )

        def relu(c):
            hid[c] = keep.tile([P, TC, PACK], BF16, name="hid_%d" % c, align_bytes=64)
            nc.scalar.activation(out=hid[c][:], in_=less[c][:].rearrange("p j t -> p t j"), func=ACT.Relu)

        def less_mean_packed(c, cols):
            groups = slice(cols.start // GROUP, cols.stop // GROUP)
            count = groups.stop - groups.start
            nc.vector.tensor_tensor(
                out=less[c][:, cols, :].rearrange("p (b i) j -> p b i j", i=GROUP),
                in0=a_bank[c, 0].rearrange("p (j b) i -> p b i j", j=PACK)[:, groups, :, :],
                in1=sums[c, 0][:].rearrange("p (b j) -> p b j", j=PACK)[:, groups, :]
                .unsqueeze(2)
                .to_broadcast([P, count, GROUP, PACK]),
                op=ALU.add,
            )

        def relu_packed(c, cols):
            nc.vector.tensor_scalar_max(out=hid[c][:, cols, :], in0=less[c][:, cols, :], scalar1=0.0)

        def quantize(c, parts):
            codes[c] = keep.tile([P, TC], U32, name="codes_%d" % c, align_bytes=64)
            hid_plane[c] = keep.tile([P, TC], U8, name="hid_plane_%d" % c, align_bytes=64)
            for cols in parts:
                nc.vector.quantize_mx(
                    out=codes[c][:, cols].bitcast(FP8X4),
                    scales=hid_plane[c][:, cols],
                    in_=hid[c][:, cols, :].rearrange("p t j -> p (t j)"),
                )

        def open_result(c, tags):
            per_bank = N_TILES // len(tags)
            y_parts[c] = []
            for h, tag in enumerate(tags):
                bank = psum.tile([P, PACK, TC], F32, name="y_%d_%d" % (c, h), tag=tag)
                y_parts[c].append((bank, range(per_bank * h, per_bank * (h + 1))))

        def skip(c, z):
            for bank, tiles in y_parts[c]:
                for i in tiles:
                    nc.tensor.matmul_mx(
                        out=bank[:, i - tiles[0], :],
                        lhsT=wy[:, z, 2 * P * i : 2 * P * (i + 1)].bitcast(FP4X4),
                        lhsT_scale=wy_plane[:, z, P * i : P * (i + 1)],
                        start=(z == 0 and i == tiles[0]),
                        stop=False,
                        **xt_pass(z, c),
                    )

        def second_layer(c):
            for bank, tiles in y_parts[c]:
                for i in tiles:
                    nc.tensor.matmul_mx(
                        out=bank[:, i - tiles[0], :],
                        lhsT=wb[:, 4 * P * i : 4 * P * (i + 1)].bitcast(FP8X4),
                        lhsT_scale=wb_plane[:, 0, P * i : P * (i + 1)],
                        rhs=codes[c][:].bitcast(FP8X4),
                        rhs_scale=hid_plane[c][:],
                        start=False,
                        stop=(i == tiles[-1]),
                    )

        def store(c):
            for h, (bank, tiles) in enumerate(y_parts[c]):
                res = keep.tile([P, len(tiles), TC], F32, name="res_%d_%d" % (c, h))
                if h % 2 == 0:
                    nc.scalar.copy(out=res[:], in_=bank[:, 0 : len(tiles), :])
                else:
                    nc.vector.tensor_copy(out=res[:], in_=bank[:, 0 : len(tiles), :])
                queue = nc.scalar if h == 2 else nc.sync
                queue.dma_start(out=out_by_tile[:, tiles[0] : tiles[-1] + 1, TC * c : TC * (c + 1)], in_=res[:])

        all_cols = [slice(0, TC)]
        halves = [slice(0, TC // 2), slice(TC // 2, TC)]
        low, high, whole = range(0, 2), range(2, 4), range(4)
        first_layer(0, low)
        first_layer(0, high)
        first_layer(1, whole)
        first_layer(3, whole)
        first_layer(2, whole)
        open_result(0, ["y_0"])
        skip(0, 0)
        skip(0, 1)
        group_sums(0, low)
        group_sums(0, high)
        less_mean(0, low)
        less_mean(0, high)
        relu(0)
        group_sums_by_halves(3)
        group_sums(1, whole)
        quantize(0, all_cols)
        second_layer(0)
        less_mean(1, whole)
        relu(1)
        store(0)
        open_result(1, ["y_1"])
        skip(1, 0)
        skip(1, 1)
        open_result(2, ["y_2", "a_0_0"])
        skip(2, 0)
        skip(2, 1)
        group_sums(2, whole)
        less_mean(2, whole)
        relu(2)
        quantize(1, all_cols)
        second_layer(1)
        store(1)
        open_result(3, ["a_0_2", "a_1_0", "a_2_0", "y_0"])
        skip(3, 0)
        skip(3, 1)
        less[3] = keep.tile([P, TC, PACK], BF16, name="less_3", align_bytes=64)
        hid[3] = keep.tile([P, TC, PACK], BF16, name="hid_3", align_bytes=64)
        less_mean_packed(3, halves[0])
        less_mean_packed(3, halves[1])
        relu_packed(3, halves[0])
        quantize(2, all_cols)
        second_layer(2)
        relu_packed(3, halves[1])
        quantize(3, halves)
        second_layer(3)
        store(2)
        store(3)
